import numpy as np
import ml_dtypes


def mxq(x, axis, fmt="e4m3"):
    dtype, down = {"e4m3": (ml_dtypes.float8_e4m3fn, 7), "e5m2": (ml_dtypes.float8_e5m2, 14)}[fmt]
    v = np.moveaxis(np.asarray(x, np.float32).astype(ml_dtypes.bfloat16).astype(np.float64), axis, -1)
    blocks = v.reshape(v.shape[:-1] + (-1, 32))
    amax = np.abs(blocks).max(-1, keepdims=True)
    byte = np.maximum(np.where(amax > 0, np.frexp(amax)[1] - 1 + 127, 0) - down, 1)
    scale = np.exp2(byte - 127.0)
    codes = (blocks / scale).astype(np.float32).astype(dtype).astype(np.float64)
    return np.moveaxis((codes * scale).reshape(v.shape), -1, axis)


WIDE = False


def mx_kscale(k):
    if not WIDE:
        return np.ones(k)
    levels = np.array([10, -10, 5, -5, 0])
    if k % 512:
        return np.exp2(np.random.permutation(np.resize(levels, k // 32))).repeat(32)
    a = np.empty((k // 512, 16))
    for p in range(k // 512):
        a[p, :8] = np.random.permutation(np.resize(levels, 8))
        for g in range(8):
            far = levels[np.abs(levels - a[p, g]) >= 10]
            a[p, g + 8] = far[np.random.randint(len(far))]
    return np.exp2(a.ravel()).repeat(32)


def f64(x):
    return np.asarray(x).astype(np.float64)


def striped8(idx):
    return np.asarray(idx).reshape(8, -1, 16).transpose(0, 2, 1).reshape(128, -1).astype(np.uint16)


def unstriped8(offs):
    return offs.reshape(8, 16, -1).transpose(0, 2, 1).reshape(8, -1).astype(np.int64)


def pick8(x, idx, run):
    r = np.arange(len(x))
    return x[r[:, None], idx[r % (8 * run) // run]]


E2M1 = np.array([0.0, 0.5, 1.0, 1.5, 2.0, 3.0, 4.0, 6.0, -0.0, -0.5, -1.0, -1.5, -2.0, -3.0, -4.0, -6.0])


def pack_weight(w, fmt):
    k, n = w.shape
    w = f64(np.asarray(w, np.float32).astype(ml_dtypes.bfloat16)).reshape(k // 32, 32, n)
    amax = np.abs(w).max(1)
    if fmt == "e4m3":
        byte = np.frexp(amax)[1] - 1 + 127 - 7
    else:
        mant, ex = np.frexp(amax / 6.0)
        byte = np.where(mant > 0.5, ex, ex - 1) + 127
    byte = np.clip(np.where(amax > 0, byte, 1), 1, 254)
    scaled = (w * np.exp2(127.0 - byte)[:, None, :]).reshape(k, n).astype(np.float32)
    by_word = np.ascontiguousarray(scaled.reshape(k // 512, 128, 4, n).transpose(0, 1, 3, 2))
    if fmt == "e4m3":
        words = by_word.astype(ml_dtypes.float8_e4m3fn).view(np.uint8)
    else:
        c = by_word.astype(ml_dtypes.float4_e2m1fn).view(np.uint8) & 0xF
        words = (c[..., 0::2] | (c[..., 1::2] << 4)).reshape(k // 512, 128, 2 * n)
    return np.ascontiguousarray(words), np.ascontiguousarray(byte.astype(np.uint8).reshape(k // 512, 16, n))


def unpack_weight(words, scales, fmt):
    g, _, n = scales.shape
    words = np.ascontiguousarray(words).reshape(g, 128, n, -1)
    if fmt == "e4m3":
        vals = words.view(ml_dtypes.float8_e4m3fn).astype(np.float64)
    else:
        nib = np.empty((g, 128, n, 4), np.uint8)
        nib[..., 0::2] = words & 0xF
        nib[..., 1::2] = words >> 4
        vals = E2M1[nib]
    vals = vals * np.repeat(np.exp2(scales.astype(np.float64) - 127.0), 8, axis=1)[..., None]
    return vals.transpose(0, 1, 3, 2).reshape(g * 512, n)


D, E, T, Q, I = 512, 512, 1024, 128, 512


def setup_inputs():
    n = np.random.standard_normal
    idx = np.stack([np.random.permutation(T)[:I] for _ in range(8)])
    idx2 = np.stack([np.random.permutation(T)[:I] for _ in range(8)])
    fd = mx_kscale(D)
    fe = mx_kscale(E)
    keysp = pack_weight(n((D, T)) / fd[:, None], "e2m1")
    return {
        "query": (n((D, Q)) * 0.5 / np.sqrt(D) * fd[:, None]).astype(np.float32),
        "keys_words": keysp[0],
        "keys_scales": keysp[1],
        "gout": (n((E, Q)) * 1 / np.sqrt(E) * fe[:, None]).astype(np.float32),
        "vals": (n((E, T)) / fe[:, None]).astype(np.float32),
        "lam": (np.random.uniform(0.3, 1.2, (Q, 1))).astype(np.float32),
        "share": (np.random.uniform(0.3, 1.0, (Q, 1))).astype(np.float32),
        "offs": striped8(idx),
        "offs2": striped8(idx2),
    }


def reference(query, keys_words, keys_scales, gout, vals, lam, share, offs, offs2):
    idx = unstriped8(offs)
    idx2 = unstriped8(offs2)
    keysu = unpack_weight(keys_words, keys_scales, "e2m1")
    queryq = mxq(f64(query), 0, "e4m3")
    a = queryq.T @ keysu
    goutq = mxq(f64(gout), 0, "e4m3")
    valsq = mxq(f64(vals), 0, "e4m3")
    dw = goutq.T @ valsq
    s = pick8(a, idx, 16) + pick8(a, idx2, 16) * f64(lam)
    p = np.exp(s - np.max(s, axis=1, keepdims=True))
    w = p / np.sum(p, axis=1, keepdims=True) * 512.0
    dj = pick8(dw, idx, 16) + pick8(dw, idx2, 16) * f64(share)
    mw = np.sum(w * dj, axis=1, keepdims=True) / 512.0
    ds = w * (dj - mw)
    da = np.zeros((Q, T))
    da[np.arange(Q)[:, None], idx[np.arange(Q) % 128 // 16]] = ds
    db = np.zeros((Q, T))
    db[np.arange(Q)[:, None], idx2[np.arange(Q) % 128 // 16]] = ds
    y = da + db * f64(lam)
    return y

@@ -1,0 +1,202 @@
+from contextlib import ExitStack
+
+import concourse.mybir as mybir
+
+D, E, T, Q, SLOTS = 512, 512, 1024, 128, 512
+FLOPS = 2 * Q * T * (D + E)
+
+F32 = mybir.dt.float32
+BF16 = mybir.dt.bfloat16
+I32 = mybir.dt.int32
+U32 = mybir.dt.uint32
+U16 = mybir.dt.uint16
+U8 = mybir.dt.uint8
+FP8X4 = mybir.dt.float8_e4m3fn_x4
+FP4X4 = mybir.dt.float4_e2m1fn_x4
+ALU = mybir.AluOpType
+ACT = mybir.ActivationFunctionType
+AX = mybir.AxisListType
+
+P = 128
+PACK = 4
+BANK = 512
+HALF = SLOTS // 2
+LIST_COLS = SLOTS // 16
+
+VAL_LOADS = (
+    (384, ((256, "scalar", "scalar"), (128, "scalar", "scalar"))),
+    (384, ((256, "scalar", "scalar"), (128, "vector", "scalar"))),
+    (256, ((128, "vector", "scalar"), (128, "vector", "vector"))),
+)
+OUT_PIECES = (384, 384, 256)
+
+
+def tile_attend_gpairs_heads_kernel(tc, query, keys_words, keys_scales, gout, vals, lam, share, offs, offs2, out):
+    nc = tc.nc
+
+    def copy_on(engine, dst, src):
+        if engine == "scalar":
+            nc.scalar.copy(out=dst, in_=src)
+        else:
+            nc.vector.tensor_copy(out=dst, in_=src)
+
+    with ExitStack() as ctx:
+        keep = ctx.enter_context(tc.tile_pool(name="keep", bufs=1))
+        psum = ctx.enter_context(tc.psum_pool(name="psum", bufs=1))
+
+        def quantise(name, raw_cols, width, engine):
+            grouped = keep.tile([P, width, PACK], BF16, align_bytes=64, name=name + "_bf")
+            codes = keep.tile([P, width], U32, align_bytes=64, name=name + "_codes")
+            scales = keep.tile([P, width], U8, align_bytes=64, name=name + "_scales")
+            copy_on(
+                engine,
+                grouped[:].rearrange("p (c i) t -> p c t i", i=4),
+                raw_cols.rearrange("p t (c i) -> p c t i", i=4),
+            )
+            nc.vector.quantize_mx(
+                out=codes[:].bitcast(FP8X4), scales=scales[:], in_=grouped[:].rearrange("p w t -> p (w t)")
+            )
+            return codes, scales
+
+        list1 = keep.tile([P, LIST_COLS], U16, name="list1")
+        list2 = keep.tile([P, LIST_COLS], U16, name="list2")
+        nc.sync.dma_start(list2[:], offs2)
+        nc.sync.dma_start(list1[:], offs)
+        q_raw = keep.tile([P, PACK, Q], F32, name="q_raw")
+        nc.sync.dma_start(out=q_raw[:], in_=query.rearrange("(p t) q -> p t q", t=PACK))
+        key_words = keep.tile([P, 2 * T], U8, align_bytes=64, name="key_words")
+        nc.sync.dma_start(out=key_words[:].bitcast(I32), in_=keys_words[0].bitcast(I32))
+        key_scales = keep.tile([P, T], U8, align_bytes=64, name="key_scales")
+        for quad in range(4):
+            nc.scalar.dma_start(
+                out=key_scales[32 * quad : 32 * quad + 4, :].bitcast(I32),
+                in_=keys_scales[0, 4 * quad : 4 * quad + 4, :].bitcast(I32),
+            )
+        g_raw = keep.tile([P, PACK, Q], F32, name="g_raw")
+        nc.sync.dma_start(out=g_raw[:], in_=gout.rearrange("(p t) q -> p t q", t=PACK))
+        vals_rows = vals.rearrange("(p t) c -> p t c", t=PACK)
+        v_raw = []
+        col = 0
+        for n, (width, pieces) in enumerate(VAL_LOADS):
+            raw = keep.tile([P, PACK, width], F32, name="v_raw%d" % n)
+            nc.sync.dma_start(out=raw[:], in_=vals_rows[:, :, col : col + width])
+            v_raw.append(raw)
+            col = col + width
+        lam_col = keep.tile([P, 1], F32, name="lam_col")
+        share_col = keep.tile([P, 1], F32, name="share_col")
+        nc.scalar.dma_start(out=lam_col[:], in_=lam)
+        nc.scalar.dma_start(out=share_col[:], in_=share)
+
+        ones = keep.tile([P, SLOTS], F32, name="ones")
+        nc.vector.memset(ones[:], 1.0)
+        warm = keep.tile([P, 1], F32, name="warm")
+        nc.scalar.activation(out=warm[:], in_=ones[:, 0:1], func=ACT.Exp)
+        da = keep.tile([P, T], F32, name="da")
+        db = keep.tile([P, T], F32, name="db")
+        nc.vector.memset(da[:], 0.0)
+        nc.vector.memset(db[:], 0.0)
+
+        q_codes, q_scales = quantise("q", q_raw[:], Q, "vector")
+        a = keep.tile([P, T], F32, name="a")
+        for b, engine in enumerate(("scalar", "vector")):
+            bank = psum.tile([P, BANK], F32, name="a_bank%d" % b)
+            nc.tensor.matmul_mx(
+                out=bank[:],
+                lhsT=q_codes[:].bitcast(FP8X4),
+                lhsT_scale=q_scales[:],
+                rhs=key_words[:, 2 * BANK * b : 2 * BANK * (b + 1)].bitcast(FP4X4),
+                rhs_scale=key_scales[:, BANK * b : BANK * (b + 1)],
+                start=True,
+                stop=True,
+            )
+            copy_on(engine, a[:, BANK * b : BANK * (b + 1)], bank[:])
+        lam_wide = keep.tile([P, SLOTS], F32, name="lam_wide")
+        share_wide = keep.tile([P, SLOTS], F32, name="share_wide")
+        nc.vector.tensor_scalar(out=lam_wide[:], in0=ones[:], scalar1=lam_col[:], scalar2=None, op0=ALU.mult)
+        nc.vector.tensor_scalar(out=share_wide[:], in0=ones[:], scalar1=share_col[:], scalar2=None, op0=ALU.mult)
+        g_codes, g_scales = quantise("g", g_raw[:], Q, "vector")
+
+        halves = [(slice(HALF * h, HALF * (h + 1)), slice(LIST_COLS // 2 * h, LIST_COLS // 2 * (h + 1))) for h in range(2)]
+
+        def join_pair(name, window, factor_wide):
+            second = keep.tile([P, SLOTS], F32, name=name + "_second")
+            joined = keep.tile([P, SLOTS], F32, name=name)
+            for slots, cols in halves:
+                nc.vector.tensor_tensor(
+                    second[:, slots], window[:].indirect(list2[:, cols]), factor_wide[:, slots], ALU.mult
+                )
+            for slots, cols in halves:
+                nc.vector.tensor_tensor(joined[:, slots], window[:].indirect(list1[:, cols]), second[:, slots], ALU.add)
+            return joined
+
+        s = join_pair("s", a, lam_wide)
+        neg_max = keep.tile([P, 1], F32, name="neg_max")
+        nc.vector.tensor_reduce(out=neg_max[:], in_=s[:], axis=AX.X, op=ALU.max, negate=True)
+        p = keep.tile([P, SLOTS], F32, name="p")
+        p_sum = keep.tile([P, 1], F32, name="p_sum")
+        nc.scalar.activation(out=p[:], in_=s[:], func=ACT.Exp, bias=neg_max[:], accum_out=p_sum[:])
+
+        dw = keep.tile([P, T], F32, name="dw")
+        col = 0
+        for n, (width, pieces) in enumerate(VAL_LOADS):
+            inner = 0
+            for m, (piece, cast_engine, out_engine) in enumerate(pieces):
+                v_codes, v_scales = quantise("v%d_%d" % (n, m), v_raw[n][:, :, inner : inner + piece], piece, cast_engine)
+                bank = psum.tile([P, piece], F32, name="dw_bank%d_%d" % (n, m))
+                nc.tensor.matmul_mx(
+                    out=bank[:],
+                    lhsT=g_codes[:].bitcast(FP8X4),
+                    lhsT_scale=g_scales[:],
+                    rhs=v_codes[:].bitcast(FP8X4),
+                    rhs_scale=v_scales[:],
+                    start=True,
+                    stop=True,
+                )
+                copy_on(out_engine, dw[:, col : col + piece], bank[:])
+                inner = inner + piece
+                col = col + piece
+
+        inv_sum = keep.tile([P, 1], F32, name="inv_sum")
+        nc.vector.reciprocal(out=inv_sum[:], in_=p_sum[:])
+        w_scale = keep.tile([P, 1], F32, name="w_scale")
+        nc.scalar.activation(out=w_scale[:], in_=inv_sum[:], func=ACT.Copy, scale=float(SLOTS))
+        w = keep.tile([P, SLOTS], F32, name="w")
+        nc.scalar.activation(out=w[:], in_=p[:], func=ACT.Copy, scale=w_scale[:])
+        w_lam = keep.tile([P, SLOTS], F32, name="w_lam")
+        nc.scalar.activation(out=w_lam[:], in_=w[:], func=ACT.Copy, scale=lam_col[:])
+
+        dj = join_pair("dj", dw, share_wide)
+        mw_parts = keep.tile([P, 2], F32, name="mw_parts")
+        weighted = keep.tile([P, SLOTS], F32, name="weighted")
+        for h, (slots, cols) in enumerate(halves):
+            nc.vector.scalar_tensor_tensor(
+                out=weighted[:, slots],
+                in0=dj[:, slots],
+                scalar=1.0 / SLOTS,
+                in1=w[:, slots],
+                op0=ALU.mult,
+                op1=ALU.mult,
+                accum_out=mw_parts[:, h : h + 1],
+            )
+        centred = keep.tile([P, SLOTS], F32, name="centred")
+        for slots, cols in halves:
+            nc.vector.tensor_scalar(
+                out=centred[:, slots],
+                in0=dj[:, slots],
+                scalar1=mw_parts[:, 0:1],
+                scalar2=mw_parts[:, 1:2],
+                op0=ALU.subtract,
+                op1=ALU.subtract,
+            )
+        for slots, cols in halves:
+            nc.vector.tensor_tensor(da[:].indirect(list1[:, cols]), centred[:, slots], w[:, slots], ALU.mult)
+            nc.vector.tensor_tensor(db[:].indirect(list2[:, cols]), centred[:, slots], w_lam[:, slots], ALU.mult)
+
+        col = 0
+        for n, width in enumerate(OUT_PIECES):
+            cols = slice(col, col + width)
+            y = keep.tile([P, width], F32, name="y%d" % n)
+            nc.vector.tensor_tensor(y[:], da[:, cols], db[:, cols], ALU.add)
+            queue = nc.scalar if n % 2 else nc.sync
+            queue.dma_start(out=out[:, cols], in_=y[:])
+            col = col + width

@@ -19,14 +19,15 @@ AX = mybir.AxisListType
 
 P = 128
 PACK = 4
-BANK = 512
+KEY_PIECE = 256
 HALF = SLOTS // 2
 LIST_COLS = SLOTS // 16
 
 VAL_LOADS = (
-    (384, ((256, "scalar", "scalar"), (128, "scalar", "scalar"))),
-    (384, ((256, "scalar", "scalar"), (128, "vector", "scalar"))),
-    (256, ((128, "vector", "scalar"), (128, "vector", "vector"))),
+    (256, ((256, "scalar", "scalar"),)),
+    (256, ((256, "scalar", "scalar"),)),
+    (256, ((256, "scalar", "scalar"),)),
+    (256, ((128, "vector", "scalar"), (128, "scalar", "scalar"))),
 )
 OUT_PIECES = (384, 384, 256)
 
@@ -45,7 +46,7 @@ def tile_attend_gpairs_heads_kernel(tc, query, keys_words, keys_scales, gout, va
         psum = ctx.enter_context(tc.psum_pool(name="psum", bufs=1))
 
         def quantise(name, raw_cols, width, engine):
-            grouped = keep.tile([P, width, PACK], BF16, align_bytes=64, name=name + "_bf")
+            grouped = keep.tile([P, width, PACK], BF16, align_bytes=64, name=name + "_bf", tag=name + "_bf")
             codes = keep.tile([P, width], U32, align_bytes=64, name=name + "_codes")
             scales = keep.tile([P, width], U8, align_bytes=64, name=name + "_scales")
             copy_on(
@@ -61,9 +62,9 @@ def tile_attend_gpairs_heads_kernel(tc, query, keys_words, keys_scales, gout, va
         list1 = keep.tile([P, LIST_COLS], U16, name="list1")
         list2 = keep.tile([P, LIST_COLS], U16, name="list2")
         nc.sync.dma_start(list2[:], offs2)
-        nc.sync.dma_start(list1[:], offs)
         q_raw = keep.tile([P, PACK, Q], F32, name="q_raw")
         nc.sync.dma_start(out=q_raw[:], in_=query.rearrange("(p t) q -> p t q", t=PACK))
+        nc.sync.dma_start(list1[:], offs)
         key_words = keep.tile([P, 2 * T], U8, align_bytes=64, name="key_words")
         nc.sync.dma_start(out=key_words[:].bitcast(I32), in_=keys_words[0].bitcast(I32))
         key_scales = keep.tile([P, T], U8, align_bytes=64, name="key_scales")
@@ -73,14 +74,15 @@ def tile_attend_gpairs_heads_kernel(tc, query, keys_words, keys_scales, gout, va
                 in_=keys_scales[0, 4 * quad : 4 * quad + 4, :].bitcast(I32),
             )
         g_raw = keep.tile([P, PACK, Q], F32, name="g_raw")
-        nc.sync.dma_start(out=g_raw[:], in_=gout.rearrange("(p t) q -> p t q", t=PACK))
         vals_rows = vals.rearrange("(p t) c -> p t c", t=PACK)
         v_raw = []
         col = 0
         for n, (width, pieces) in enumerate(VAL_LOADS):
-            raw = keep.tile([P, PACK, width], F32, name="v_raw%d" % n)
+            raw = keep.tile([P, PACK, width], F32, name="v_raw%d" % n, tag="v_raw%d" % n)
             nc.sync.dma_start(out=raw[:], in_=vals_rows[:, :, col : col + width])
             v_raw.append(raw)
+            if n == 0:
+                nc.sync.dma_start(out=g_raw[:], in_=gout.rearrange("(p t) q -> p t q", t=PACK))
             col = col + width
         lam_col = keep.tile([P, 1], F32, name="lam_col")
         share_col = keep.tile([P, 1], F32, name="share_col")
@@ -98,29 +100,29 @@ def tile_attend_gpairs_heads_kernel(tc, query, keys_words, keys_scales, gout, va
 
         q_codes, q_scales = quantise("q", q_raw[:], Q, "vector")
         a = keep.tile([P, T], F32, name="a")
-        for b, engine in enumerate(("scalar", "vector")):
-            bank = psum.tile([P, BANK], F32, name="a_bank%d" % b)
+        for b in range(T // KEY_PIECE):
+            bank = psum.tile([P, KEY_PIECE], F32, name="a_bank%d" % b, tag="bank%d" % b)
             nc.tensor.matmul_mx(
                 out=bank[:],
                 lhsT=q_codes[:].bitcast(FP8X4),
                 lhsT_scale=q_scales[:],
-                rhs=key_words[:, 2 * BANK * b : 2 * BANK * (b + 1)].bitcast(FP4X4),
-                rhs_scale=key_scales[:, BANK * b : BANK * (b + 1)],
+                rhs=key_words[:, 2 * KEY_PIECE * b : 2 * KEY_PIECE * (b + 1)].bitcast(FP4X4),
+                rhs_scale=key_scales[:, KEY_PIECE * b : KEY_PIECE * (b + 1)],
                 start=True,
                 stop=True,
             )
-            copy_on(engine, a[:, BANK * b : BANK * (b + 1)], bank[:])
+            nc.vector.tensor_copy(out=a[:, KEY_PIECE * b : KEY_PIECE * (b + 1)], in_=bank[:])
         lam_wide = keep.tile([P, SLOTS], F32, name="lam_wide")
         share_wide = keep.tile([P, SLOTS], F32, name="share_wide")
         nc.vector.tensor_scalar(out=lam_wide[:], in0=ones[:], scalar1=lam_col[:], scalar2=None, op0=ALU.mult)
         nc.vector.tensor_scalar(out=share_wide[:], in0=ones[:], scalar1=share_col[:], scalar2=None, op0=ALU.mult)
-        g_codes, g_scales = quantise("g", g_raw[:], Q, "vector")
+        g_codes, g_scales = quantise("g", g_raw[:], Q, "scalar")
 
         halves = [(slice(HALF * h, HALF * (h + 1)), slice(LIST_COLS // 2 * h, LIST_COLS // 2 * (h + 1))) for h in range(2)]
 
-        def join_pair(name, window, factor_wide):
+        def join_pair(name, window, factor_wide, tag):
             second = keep.tile([P, SLOTS], F32, name=name + "_second")
-            joined = keep.tile([P, SLOTS], F32, name=name)
+            joined = keep.tile([P, SLOTS], F32, name=name, tag=tag)
             for slots, cols in halves:
                 nc.vector.tensor_tensor(
                     second[:, slots], window[:].indirect(list2[:, cols]), factor_wide[:, slots], ALU.mult
@@ -129,20 +131,15 @@ def tile_attend_gpairs_heads_kernel(tc, query, keys_words, keys_scales, gout, va
                 nc.vector.tensor_tensor(joined[:, slots], window[:].indirect(list1[:, cols]), second[:, slots], ALU.add)
             return joined
 
-        s = join_pair("s", a, lam_wide)
-        neg_max = keep.tile([P, 1], F32, name="neg_max")
-        nc.vector.tensor_reduce(out=neg_max[:], in_=s[:], axis=AX.X, op=ALU.max, negate=True)
-        p = keep.tile([P, SLOTS], F32, name="p")
-        p_sum = keep.tile([P, 1], F32, name="p_sum")
-        nc.scalar.activation(out=p[:], in_=s[:], func=ACT.Exp, bias=neg_max[:], accum_out=p_sum[:])
+        s = join_pair("s", a, lam_wide, "s")
 
-        dw = keep.tile([P, T], F32, name="dw")
+        dw = keep.tile([P, T], F32, name="dw", tag="v_raw%d" % (len(VAL_LOADS) - 1))
         col = 0
         for n, (width, pieces) in enumerate(VAL_LOADS):
             inner = 0
             for m, (piece, cast_engine, out_engine) in enumerate(pieces):
                 v_codes, v_scales = quantise("v%d_%d" % (n, m), v_raw[n][:, :, inner : inner + piece], piece, cast_engine)
-                bank = psum.tile([P, piece], F32, name="dw_bank%d_%d" % (n, m))
+                bank = psum.tile([P, piece], F32, name="dw_bank%d_%d" % (n, m), tag="bank%d" % ((4 + n + m) % 8))
                 nc.tensor.matmul_mx(
                     out=bank[:],
                     lhsT=g_codes[:].bitcast(FP8X4),
@@ -156,24 +153,28 @@ def tile_attend_gpairs_heads_kernel(tc, query, keys_words, keys_scales, gout, va
                 inner = inner + piece
                 col = col + piece
 
-        inv_sum = keep.tile([P, 1], F32, name="inv_sum")
-        nc.vector.reciprocal(out=inv_sum[:], in_=p_sum[:])
-        w_scale = keep.tile([P, 1], F32, name="w_scale")
-        nc.scalar.activation(out=w_scale[:], in_=inv_sum[:], func=ACT.Copy, scale=float(SLOTS))
+        neg_max = keep.tile([P, 1], F32, align_bytes=64, name="neg_max", tag="v%d_1_bf" % (len(VAL_LOADS) - 1))
+        nc.vector.tensor_reduce(out=neg_max[:], in_=s[:], axis=AX.X, op=ALU.max, negate=True)
+        p = keep.tile([P, SLOTS], F32, name="p")
+        sums = keep.tile([P, 2], F32, name="sums", tag="sums")
+        nc.scalar.activation(out=p[:], in_=s[:], func=ACT.Exp, bias=neg_max[:], accum_out=sums[:, 0:1])
+        nc.scalar.activation(out=sums[:, 1:2], in_=sums[:, 0:1], func=ACT.Copy, scale=1.0 / SLOTS)
+        inv = keep.tile([P, 2], F32, name="inv")
+        nc.vector.reciprocal(out=inv[:], in_=sums[:])
         w = keep.tile([P, SLOTS], F32, name="w")
-        nc.scalar.activation(out=w[:], in_=p[:], func=ACT.Copy, scale=w_scale[:])
+        nc.scalar.activation(out=w[:], in_=p[:], func=ACT.Copy, scale=inv[:, 1:2])
         w_lam = keep.tile([P, SLOTS], F32, name="w_lam")
         nc.scalar.activation(out=w_lam[:], in_=w[:], func=ACT.Copy, scale=lam_col[:])
 
-        dj = join_pair("dj", dw, share_wide)
+        dj = join_pair("dj", dw, share_wide, "sums")
         mw_parts = keep.tile([P, 2], F32, name="mw_parts")
         weighted = keep.tile([P, SLOTS], F32, name="weighted")
         for h, (slots, cols) in enumerate(halves):
             nc.vector.scalar_tensor_tensor(
                 out=weighted[:, slots],
                 in0=dj[:, slots],
-                scalar=1.0 / SLOTS,
-                in1=w[:, slots],
+                scalar=inv[:, 0:1],
+                in1=p[:, slots],
                 op0=ALU.mult,
                 op1=ALU.mult,
                 accum_out=mw_parts[:, h : h + 1],

@@ -19,7 +19,7 @@ AX = mybir.AxisListType
 
 P = 128
 PACK = 4
-KEY_PIECE = 256
+KEY_PIECES = ((256, "scalar"), (256, "scalar"), (256, "vector"), (128, "vector"), (128, "vector"))
 HALF = SLOTS // 2
 LIST_COLS = SLOTS // 16
 
@@ -29,7 +29,7 @@ VAL_LOADS = (
     (256, ((256, "scalar", "scalar"),)),
     (256, ((128, "vector", "scalar"), (128, "scalar", "scalar"))),
 )
-OUT_PIECES = (384, 384, 256)
+OUT_PIECES = (256, 256, 256, 256)
 
 
 def tile_attend_gpairs_heads_kernel(tc, query, keys_words, keys_scales, gout, vals, lam, share, offs, offs2, out):
@@ -61,18 +61,20 @@ def tile_attend_gpairs_heads_kernel(tc, query, keys_words, keys_scales, gout, va
 
         list1 = keep.tile([P, LIST_COLS], U16, name="list1")
         list2 = keep.tile([P, LIST_COLS], U16, name="list2")
-        nc.sync.dma_start(list2[:], offs2)
-        q_raw = keep.tile([P, PACK, Q], F32, name="q_raw")
-        nc.sync.dma_start(out=q_raw[:], in_=query.rearrange("(p t) q -> p t q", t=PACK))
-        nc.sync.dma_start(list1[:], offs)
-        key_words = keep.tile([P, 2 * T], U8, align_bytes=64, name="key_words")
-        nc.sync.dma_start(out=key_words[:].bitcast(I32), in_=keys_words[0].bitcast(I32))
         key_scales = keep.tile([P, T], U8, align_bytes=64, name="key_scales")
+        q_raw = keep.tile([P, PACK, Q], F32, name="q_raw")
         for quad in range(4):
-            nc.scalar.dma_start(
+            nc.sync.dma_start(
                 out=key_scales[32 * quad : 32 * quad + 4, :].bitcast(I32),
                 in_=keys_scales[0, 4 * quad : 4 * quad + 4, :].bitcast(I32),
             )
+            if quad == 0:
+                nc.sync.dma_start(out=q_raw[:], in_=query.rearrange("(p t) q -> p t q", t=PACK))
+        key_words = keep.tile([P, 2 * T], U8, align_bytes=64, name="key_words")
+        nc.sync.dma_start(out=key_words[:].bitcast(I32), in_=keys_words[0].bitcast(I32))
+        lam_col = keep.tile([P, 1], F32, name="lam_col")
+        share_col = keep.tile([P, 1], F32, name="share_col")
+        nc.sync.dma_start(out=lam_col[:], in_=lam)
         g_raw = keep.tile([P, PACK, Q], F32, name="g_raw")
         vals_rows = vals.rearrange("(p t) c -> p t c", t=PACK)
         v_raw = []
@@ -82,12 +84,11 @@ def tile_attend_gpairs_heads_kernel(tc, query, keys_words, keys_scales, gout, va
             nc.sync.dma_start(out=raw[:], in_=vals_rows[:, :, col : col + width])
             v_raw.append(raw)
             if n == 0:
+                nc.sync.dma_start(list2[:], offs2)
+                nc.sync.dma_start(list1[:], offs)
                 nc.sync.dma_start(out=g_raw[:], in_=gout.rearrange("(p t) q -> p t q", t=PACK))
             col = col + width
-        lam_col = keep.tile([P, 1], F32, name="lam_col")
-        share_col = keep.tile([P, 1], F32, name="share_col")
-        nc.scalar.dma_start(out=lam_col[:], in_=lam)
-        nc.scalar.dma_start(out=share_col[:], in_=share)
+        nc.sync.dma_start(out=share_col[:], in_=share)
 
         ones = keep.tile([P, SLOTS], F32, name="ones")
         nc.vector.memset(ones[:], 1.0)
@@ -100,22 +101,22 @@ def tile_attend_gpairs_heads_kernel(tc, query, keys_words, keys_scales, gout, va
 
         q_codes, q_scales = quantise("q", q_raw[:], Q, "vector")
         a = keep.tile([P, T], F32, name="a")
-        for b in range(T // KEY_PIECE):
-            bank = psum.tile([P, KEY_PIECE], F32, name="a_bank%d" % b, tag="bank%d" % b)
+        col = 0
+        for b, (piece, engine) in enumerate(KEY_PIECES):
+            bank = psum.tile([P, piece], F32, name="a_bank%d" % b, tag="bank%d" % b)
             nc.tensor.matmul_mx(
                 out=bank[:],
                 lhsT=q_codes[:].bitcast(FP8X4),
                 lhsT_scale=q_scales[:],
-                rhs=key_words[:, 2 * KEY_PIECE * b : 2 * KEY_PIECE * (b + 1)].bitcast(FP4X4),
-                rhs_scale=key_scales[:, KEY_PIECE * b : KEY_PIECE * (b + 1)],
+                rhs=key_words[:, 2 * col : 2 * (col + piece)].bitcast(FP4X4),
+                rhs_scale=key_scales[:, col : col + piece],
                 start=True,
                 stop=True,
             )
-            nc.vector.tensor_copy(out=a[:, KEY_PIECE * b : KEY_PIECE * (b + 1)], in_=bank[:])
+            copy_on(engine, a[:, col : col + piece], bank[:])
+            col = col + piece
         lam_wide = keep.tile([P, SLOTS], F32, name="lam_wide")
-        share_wide = keep.tile([P, SLOTS], F32, name="share_wide")
         nc.vector.tensor_scalar(out=lam_wide[:], in0=ones[:], scalar1=lam_col[:], scalar2=None, op0=ALU.mult)
-        nc.vector.tensor_scalar(out=share_wide[:], in0=ones[:], scalar1=share_col[:], scalar2=None, op0=ALU.mult)
         g_codes, g_scales = quantise("g", g_raw[:], Q, "scalar")
 
         halves = [(slice(HALF * h, HALF * (h + 1)), slice(LIST_COLS // 2 * h, LIST_COLS // 2 * (h + 1))) for h in range(2)]
@@ -133,13 +134,15 @@ def tile_attend_gpairs_heads_kernel(tc, query, keys_words, keys_scales, gout, va
 
         s = join_pair("s", a, lam_wide, "s")
 
+        bank_no = len(KEY_PIECES)
         dw = keep.tile([P, T], F32, name="dw", tag="v_raw%d" % (len(VAL_LOADS) - 1))
         col = 0
         for n, (width, pieces) in enumerate(VAL_LOADS):
             inner = 0
             for m, (piece, cast_engine, out_engine) in enumerate(pieces):
                 v_codes, v_scales = quantise("v%d_%d" % (n, m), v_raw[n][:, :, inner : inner + piece], piece, cast_engine)
-                bank = psum.tile([P, piece], F32, name="dw_bank%d_%d" % (n, m), tag="bank%d" % ((4 + n + m) % 8))
+                bank = psum.tile([P, piece], F32, name="dw_bank%d_%d" % (n, m), tag="bank%d" % (bank_no % 8))
+                bank_no = bank_no + 1
                 nc.tensor.matmul_mx(
                     out=bank[:],
                     lhsT=g_codes[:].bitcast(FP8X4),
@@ -153,6 +156,8 @@ def tile_attend_gpairs_heads_kernel(tc, query, keys_words, keys_scales, gout, va
                 inner = inner + piece
                 col = col + piece
 
+        share_wide = keep.tile([P, SLOTS], F32, name="share_wide")
+        nc.vector.tensor_scalar(out=share_wide[:], in0=ones[:], scalar1=share_col[:], scalar2=None, op0=ALU.mult)
         neg_max = keep.tile([P, 1], F32, align_bytes=64, name="neg_max", tag="v%d_1_bf" % (len(VAL_LOADS) - 1))
         nc.vector.tensor_reduce(out=neg_max[:], in_=s[:], axis=AX.X, op=ALU.max, negate=True)
         p = keep.tile([P, SLOTS], F32, name="p")

from contextlib import ExitStack

import concourse.mybir as mybir

D, E, T, Q, SLOTS = 512, 512, 1024, 128, 512
FLOPS = 2 * Q * T * (D + E)

F32 = mybir.dt.float32
BF16 = mybir.dt.bfloat16
I32 = mybir.dt.int32
U32 = mybir.dt.uint32
U16 = mybir.dt.uint16
U8 = mybir.dt.uint8
FP8X4 = mybir.dt.float8_e4m3fn_x4
FP4X4 = mybir.dt.float4_e2m1fn_x4
ALU = mybir.AluOpType
ACT = mybir.ActivationFunctionType
AX = mybir.AxisListType

P = 128
PACK = 4
KEY_PIECES = ((256, "scalar"), (256, "scalar"), (256, "vector"), (128, "vector"), (128, "vector"))
HALF = SLOTS // 2
LIST_COLS = SLOTS // 16

VAL_LOADS = (
    (256, ((256, "scalar", "scalar"),)),
    (256, ((256, "scalar", "scalar"),)),
    (256, ((256, "scalar", "scalar"),)),
    (256, ((128, "vector", "scalar"), (128, "scalar", "scalar"))),
)
OUT_PIECES = (256, 256, 256, 256)


def tile_attend_gpairs_heads_kernel(tc, query, keys_words, keys_scales, gout, vals, lam, share, offs, offs2, out):
    nc = tc.nc

    def copy_on(engine, dst, src):
        if engine == "scalar":
            nc.scalar.copy(out=dst, in_=src)
        else:
            nc.vector.tensor_copy(out=dst, in_=src)

    with ExitStack() as ctx:
        keep = ctx.enter_context(tc.tile_pool(name="keep", bufs=1))
        psum = ctx.enter_context(tc.psum_pool(name="psum", bufs=1))

        def quantise(name, raw_cols, width, engine):
            grouped = keep.tile([P, width, PACK], BF16, align_bytes=64, name=name + "_bf", tag=name + "_bf")
            codes = keep.tile([P, width], U32, align_bytes=64, name=name + "_codes")
            scales = keep.tile([P, width], U8, align_bytes=64, name=name + "_scales")
            copy_on(
                engine,
                grouped[:].rearrange("p (c i) t -> p c t i", i=4),
                raw_cols.rearrange("p t (c i) -> p c t i", i=4),
            )
            nc.vector.quantize_mx(
                out=codes[:].bitcast(FP8X4), scales=scales[:], in_=grouped[:].rearrange("p w t -> p (w t)")
            )
            return codes, scales

        list1 = keep.tile([P, LIST_COLS], U16, name="list1")
        list2 = keep.tile([P, LIST_COLS], U16, name="list2")
        key_scales = keep.tile([P, T], U8, align_bytes=64, name="key_scales")
        q_raw = keep.tile([P, PACK, Q], F32, name="q_raw")
        for quad in range(4):
            nc.sync.dma_start(
                out=key_scales[32 * quad : 32 * quad + 4, :].bitcast(I32),
                in_=keys_scales[0, 4 * quad : 4 * quad + 4, :].bitcast(I32),
            )
            if quad == 0:
                nc.sync.dma_start(out=q_raw[:], in_=query.rearrange("(p t) q -> p t q", t=PACK))
        key_words = keep.tile([P, 2 * T], U8, align_bytes=64, name="key_words")
        nc.sync.dma_start(out=key_words[:].bitcast(I32), in_=keys_words[0].bitcast(I32))
        lam_col = keep.tile([P, 1], F32, name="lam_col")
        share_col = keep.tile([P, 1], F32, name="share_col")
        nc.sync.dma_start(out=lam_col[:], in_=lam)
        g_raw = keep.tile([P, PACK, Q], F32, name="g_raw")
        vals_rows = vals.rearrange("(p t) c -> p t c", t=PACK)
        v_raw = []
        col = 0
        for n, (width, pieces) in enumerate(VAL_LOADS):
            raw = keep.tile([P, PACK, width], F32, name="v_raw%d" % n, tag="v_raw%d" % n)
            nc.sync.dma_start(out=raw[:], in_=vals_rows[:, :, col : col + width])
            v_raw.append(raw)
            if n == 0:
                nc.sync.dma_start(list2[:], offs2)
                nc.sync.dma_start(list1[:], offs)
                nc.sync.dma_start(out=g_raw[:], in_=gout.rearrange("(p t) q -> p t q", t=PACK))
            col = col + width
        nc.sync.dma_start(out=share_col[:], in_=share)

        ones = keep.tile([P, SLOTS], F32, name="ones")
        nc.vector.memset(ones[:], 1.0)
        warm = keep.tile([P, 1], F32, name="warm")
        nc.scalar.activation(out=warm[:], in_=ones[:, 0:1], func=ACT.Exp)
        da = keep.tile([P, T], F32, name="da")
        db = keep.tile([P, T], F32, name="db")
        nc.vector.memset(da[:], 0.0)
        nc.vector.memset(db[:], 0.0)

        q_codes, q_scales = quantise("q", q_raw[:], Q, "vector")
        a = keep.tile([P, T], F32, name="a")
        col = 0
        for b, (piece, engine) in enumerate(KEY_PIECES):
            bank = psum.tile([P, piece], F32, name="a_bank%d" % b, tag="bank%d" % b)
            nc.tensor.matmul_mx(
                out=bank[:],
                lhsT=q_codes[:].bitcast(FP8X4),
                lhsT_scale=q_scales[:],
                rhs=key_words[:, 2 * col : 2 * (col + piece)].bitcast(FP4X4),
                rhs_scale=key_scales[:, col : col + piece],
                start=True,
                stop=True,
            )
            copy_on(engine, a[:, col : col + piece], bank[:])
            col = col + piece
        lam_wide = keep.tile([P, SLOTS], F32, name="lam_wide")
        nc.vector.tensor_scalar(out=lam_wide[:], in0=ones[:], scalar1=lam_col[:], scalar2=None, op0=ALU.mult)
        g_codes, g_scales = quantise("g", g_raw[:], Q, "scalar")

        halves = [(slice(HALF * h, HALF * (h + 1)), slice(LIST_COLS // 2 * h, LIST_COLS // 2 * (h + 1))) for h in range(2)]

        def join_pair(name, window, factor_wide, tag):
            second = keep.tile([P, SLOTS], F32, name=name + "_second")
            joined = keep.tile([P, SLOTS], F32, name=name, tag=tag)
            for slots, cols in halves:
                nc.vector.tensor_tensor(
                    second[:, slots], window[:].indirect(list2[:, cols]), factor_wide[:, slots], ALU.mult
                )
            for slots, cols in halves:
                nc.vector.tensor_tensor(joined[:, slots], window[:].indirect(list1[:, cols]), second[:, slots], ALU.add)
            return joined

        s = join_pair("s", a, lam_wide, "s")

        bank_no = len(KEY_PIECES)
        dw = keep.tile([P, T], F32, name="dw", tag="v_raw%d" % (len(VAL_LOADS) - 1))
        col = 0
        for n, (width, pieces) in enumerate(VAL_LOADS):
            inner = 0
            for m, (piece, cast_engine, out_engine) in enumerate(pieces):
                v_codes, v_scales = quantise("v%d_%d" % (n, m), v_raw[n][:, :, inner : inner + piece], piece, cast_engine)
                bank = psum.tile([P, piece], F32, name="dw_bank%d_%d" % (n, m), tag="bank%d" % (bank_no % 8))
                bank_no = bank_no + 1
                nc.tensor.matmul_mx(
                    out=bank[:],
                    lhsT=g_codes[:].bitcast(FP8X4),
                    lhsT_scale=g_scales[:],
                    rhs=v_codes[:].bitcast(FP8X4),
                    rhs_scale=v_scales[:],
                    start=True,
                    stop=True,
                )
                copy_on(out_engine, dw[:, col : col + piece], bank[:])
                inner = inner + piece
                col = col + piece

        share_wide = keep.tile([P, SLOTS], F32, name="share_wide")
        nc.vector.tensor_scalar(out=share_wide[:], in0=ones[:], scalar1=share_col[:], scalar2=None, op0=ALU.mult)
        neg_max = keep.tile([P, 1], F32, align_bytes=64, name="neg_max", tag="v%d_1_bf" % (len(VAL_LOADS) - 1))
        nc.vector.tensor_reduce(out=neg_max[:], in_=s[:], axis=AX.X, op=ALU.max, negate=True)
        p = keep.tile([P, SLOTS], F32, name="p")
        sums = keep.tile([P, 2], F32, name="sums", tag="sums")
        nc.scalar.activation(out=p[:], in_=s[:], func=ACT.Exp, bias=neg_max[:], accum_out=sums[:, 0:1])
        nc.scalar.activation(out=sums[:, 1:2], in_=sums[:, 0:1], func=ACT.Copy, scale=1.0 / SLOTS)
        inv = keep.tile([P, 2], F32, name="inv")
        nc.vector.reciprocal(out=inv[:], in_=sums[:])
        w = keep.tile([P, SLOTS], F32, name="w")
        nc.scalar.activation(out=w[:], in_=p[:], func=ACT.Copy, scale=inv[:, 1:2])
        w_lam = keep.tile([P, SLOTS], F32, name="w_lam")
        nc.scalar.activation(out=w_lam[:], in_=w[:], func=ACT.Copy, scale=lam_col[:])

        dj = join_pair("dj", dw, share_wide, "sums")
        mw_parts = keep.tile([P, 2], F32, name="mw_parts")
        weighted = keep.tile([P, SLOTS], F32, name="weighted")
        for h, (slots, cols) in enumerate(halves):
            nc.vector.scalar_tensor_tensor(
                out=weighted[:, slots],
                in0=dj[:, slots],
                scalar=inv[:, 0:1],
                in1=p[:, slots],
                op0=ALU.mult,
                op1=ALU.mult,
                accum_out=mw_parts[:, h : h + 1],
            )
        centred = keep.tile([P, SLOTS], F32, name="centred")
        for slots, cols in halves:
            nc.vector.tensor_scalar(
                out=centred[:, slots],
                in0=dj[:, slots],
                scalar1=mw_parts[:, 0:1],
                scalar2=mw_parts[:, 1:2],
                op0=ALU.subtract,
                op1=ALU.subtract,
            )
        for slots, cols in halves:
            nc.vector.tensor_tensor(da[:].indirect(list1[:, cols]), centred[:, slots], w[:, slots], ALU.mult)
            nc.vector.tensor_tensor(db[:].indirect(list2[:, cols]), centred[:, slots], w_lam[:, slots], ALU.mult)

        col = 0
        for n, width in enumerate(OUT_PIECES):
            cols = slice(col, col + width)
            y = keep.tile([P, width], F32, name="y%d" % n)
            nc.vector.tensor_tensor(y[:], da[:, cols], db[:, cols], ALU.add)
            queue = nc.scalar if n % 2 else nc.sync
            queue.dma_start(out=out[:, cols], in_=y[:])
            col = col + width
